import numpy as np
CORES = [32,33,40,41,48,49,56,57,64,65,72,73]
N = 12
GROUPS = [[0,1],[2,3],[4,5],[6,7],[8,9],[10,11]]
def setup_inputs(rng):
    return {"x": rng.standard_normal((N, 128, 4), dtype=np.float32)}
def reference(x):
    y = np.empty((N, 128, 2), x.dtype)
    for g in GROUPS:
        s = x[g].max(axis=0)
        n = len(g); b = x.shape[2] // n
        for i, r in enumerate(g):
            y[r] = s[:, i * b:(i + 1) * b]
    return {"y": y}

@@ -1,0 +1,57 @@
+from concourse.bass import DstId, RemoteDMATransfer
+
+BLOCK = 2
+
+SCRATCH = {
+    "xs": ("sbuf", [128, 2 * BLOCK], "float32"),
+    "land": ("sbuf", [128, BLOCK], "float32"),
+    "res": ("sbuf", [128, BLOCK], "float32"),
+}
+SEMAPHORES = ["loaded", "arrived", "folded", "sent", "stored"]
+
+ALU_MAX = 2
+
+
+def rank_program(g, core, T, topo):
+    rank = T.rank_of(core)
+    if rank is None:
+        return
+
+    group = [grp for grp in T.tables["GROUPS"] if rank in grp][0]
+    assert len(group) == 2
+    i = group.index(rank)
+    j = 1 - i
+    peer = T.cores[group[j]]
+    assert topo.chip(peer) == topo.chip(core)
+
+    rid, pid, _se = topo.addr(peer)
+    mask = topo.mask(core, peer)
+    n_eng = 16
+    assert mask == 0xFFFF
+
+    mine = T.xs[:, i * BLOCK:(i + 1) * BLOCK]
+    theirs = T.xs[:, j * BLOCK:(j + 1) * BLOCK]
+
+    g.sync.dma_start(T.xs[:], T.x[:]).then_inc(T.sem.loaded, 16)
+    g.wait_ge(T.sem.loaded, 16)
+
+    g.remote_dma(T.land[:], mine, T.sem.arrived, T.sem.sent, pid, rid, mask)
+
+    g.wait_ge(T.sem.arrived, n_eng)
+    g.remote_dma_fused(
+        [RemoteDMATransfer(
+            dst_ids=[DstId(rid=rid, pnc=pid)],
+            dma_engine_mask=mask,
+            remote_sem=T.sem.folded,
+            srcs=[theirs, T.land[:]],
+            dsts=[T.res[:]],
+            alu_op=ALU_MAX,
+        )],
+        local_sem=T.sem.sent,
+    )
+
+    g.sync.wait_ge(T.sem.folded, n_eng)
+    g.sync.dma_start(T.y[:], T.res[:]).then_inc(T.sem.stored, 16)
+    g.sync.wait_ge(T.sem.stored, 16)
+
+    g.wait_ge(T.sem.sent, 2 * n_eng)

@@ -3,11 +3,12 @@ from concourse.bass import DstId, RemoteDMATransfer
 BLOCK = 2
 
 SCRATCH = {
-    "xs": ("sbuf", [128, 2 * BLOCK], "float32"),
-    "land": ("sbuf", [128, BLOCK], "float32"),
-    "res": ("sbuf", [128, BLOCK], "float32"),
+    "keep": ("dram", [128, BLOCK], "float32"),
+    "give": ("dram", [128, BLOCK], "float32"),
+    "land": ("dram", [128, BLOCK], "float32"),
+    "res": ("dram", [128, BLOCK], "float32"),
 }
-SEMAPHORES = ["loaded", "arrived", "folded", "sent", "stored"]
+SEMAPHORES = ["got_keep", "got_give", "arrived", "folded", "sent", "stored"]
 
 ALU_MAX = 2
 
@@ -29,21 +30,20 @@ def rank_program(g, core, T, topo):
     n_eng = 16
     assert mask == 0xFFFF
 
-    mine = T.xs[:, i * BLOCK:(i + 1) * BLOCK]
-    theirs = T.xs[:, j * BLOCK:(j + 1) * BLOCK]
+    g.sync.dma_start(T.keep[:], T.x[:, i * BLOCK:(i + 1) * BLOCK]).then_inc(T.sem.got_keep, 16)
+    g.scalar.dma_start(T.give[:], T.x[:, j * BLOCK:(j + 1) * BLOCK]).then_inc(T.sem.got_give, 16)
 
-    g.sync.dma_start(T.xs[:], T.x[:]).then_inc(T.sem.loaded, 16)
-    g.wait_ge(T.sem.loaded, 16)
+    g.wait_ge(T.sem.got_keep, 16)
+    g.remote_dma(T.land[:], T.keep[:], T.sem.arrived, T.sem.sent, pid, rid, mask)
 
-    g.remote_dma(T.land[:], mine, T.sem.arrived, T.sem.sent, pid, rid, mask)
-
+    g.wait_ge(T.sem.got_give, 16)
     g.wait_ge(T.sem.arrived, n_eng)
     g.remote_dma_fused(
         [RemoteDMATransfer(
             dst_ids=[DstId(rid=rid, pnc=pid)],
             dma_engine_mask=mask,
             remote_sem=T.sem.folded,
-            srcs=[theirs, T.land[:]],
+            srcs=[T.give[:], T.land[:]],
             dsts=[T.res[:]],
             alu_op=ALU_MAX,
         )],

from concourse.bass import DstId, RemoteDMATransfer

BLOCK = 2

SCRATCH = {
    "keep": ("dram", [128, BLOCK], "float32"),
    "give": ("dram", [128, BLOCK], "float32"),
    "land": ("dram", [128, BLOCK], "float32"),
    "res": ("dram", [128, BLOCK], "float32"),
}
SEMAPHORES = ["got_keep", "got_give", "arrived", "folded", "sent", "stored"]

ALU_MAX = 2


def rank_program(g, core, T, topo):
    rank = T.rank_of(core)
    if rank is None:
        return

    group = [grp for grp in T.tables["GROUPS"] if rank in grp][0]
    assert len(group) == 2
    i = group.index(rank)
    j = 1 - i
    peer = T.cores[group[j]]
    assert topo.chip(peer) == topo.chip(core)

    rid, pid, _se = topo.addr(peer)
    mask = topo.mask(core, peer)
    n_eng = 16
    assert mask == 0xFFFF

    g.sync.dma_start(T.keep[:], T.x[:, i * BLOCK:(i + 1) * BLOCK]).then_inc(T.sem.got_keep, 16)
    g.scalar.dma_start(T.give[:], T.x[:, j * BLOCK:(j + 1) * BLOCK]).then_inc(T.sem.got_give, 16)

    g.wait_ge(T.sem.got_keep, 16)
    g.remote_dma(T.land[:], T.keep[:], T.sem.arrived, T.sem.sent, pid, rid, mask)

    g.wait_ge(T.sem.got_give, 16)
    g.wait_ge(T.sem.arrived, n_eng)
    g.remote_dma_fused(
        [RemoteDMATransfer(
            dst_ids=[DstId(rid=rid, pnc=pid)],
            dma_engine_mask=mask,
            remote_sem=T.sem.folded,
            srcs=[T.give[:], T.land[:]],
            dsts=[T.res[:]],
            alu_op=ALU_MAX,
        )],
        local_sem=T.sem.sent,
    )

    g.sync.wait_ge(T.sem.folded, n_eng)
    g.sync.dma_start(T.y[:], T.res[:]).then_inc(T.sem.stored, 16)
    g.sync.wait_ge(T.sem.stored, 16)

    g.wait_ge(T.sem.sent, 2 * n_eng)
